import numpy as np
import ml_dtypes


def mxq(x, axis, fmt="e4m3"):
    dtype, down = {"e4m3": (ml_dtypes.float8_e4m3fn, 7), "e5m2": (ml_dtypes.float8_e5m2, 14)}[fmt]
    v = np.moveaxis(np.asarray(x, np.float32).astype(ml_dtypes.bfloat16).astype(np.float64), axis, -1)
    blocks = v.reshape(v.shape[:-1] + (-1, 32))
    amax = np.abs(blocks).max(-1, keepdims=True)
    byte = np.maximum(np.where(amax > 0, np.frexp(amax)[1] - 1 + 127, 0) - down, 1)
    scale = np.exp2(byte - 127.0)
    codes = (blocks / scale).astype(np.float32).astype(dtype).astype(np.float64)
    return np.moveaxis((codes * scale).reshape(v.shape), -1, axis)


WIDE = False


def mx_kscale(k):
    if not WIDE:
        return np.ones(k)
    levels = np.array([10, -10, 5, -5, 0])
    if k % 512:
        return np.exp2(np.random.permutation(np.resize(levels, k // 32))).repeat(32)
    a = np.empty((k // 512, 16))
    for p in range(k // 512):
        a[p, :8] = np.random.permutation(np.resize(levels, 8))
        for g in range(8):
            far = levels[np.abs(levels - a[p, g]) >= 10]
            a[p, g + 8] = far[np.random.randint(len(far))]
    return np.exp2(a.ravel()).repeat(32)


BF16 = ml_dtypes.bfloat16


def bf(x):
    return np.asarray(x, np.float32).astype(BF16)


def f64(x):
    return np.asarray(x).astype(np.float64)


E2M1 = np.array([0.0, 0.5, 1.0, 1.5, 2.0, 3.0, 4.0, 6.0, -0.0, -0.5, -1.0, -1.5, -2.0, -3.0, -4.0, -6.0])


def pack_weight(w, fmt):
    k, n = w.shape
    w = f64(bf(w)).reshape(k // 32, 32, n)
    amax = np.abs(w).max(1)
    if fmt == "e4m3":
        byte = np.frexp(amax)[1] - 1 + 127 - 7
    else:
        mant, ex = np.frexp(amax / 6.0)
        byte = np.where(mant > 0.5, ex, ex - 1) + 127
    byte = np.clip(np.where(amax > 0, byte, 1), 1, 254)
    scaled = (w * np.exp2(127.0 - byte)[:, None, :]).reshape(k, n).astype(np.float32)
    by_word = np.ascontiguousarray(scaled.reshape(k // 512, 128, 4, n).transpose(0, 1, 3, 2))
    if fmt == "e4m3":
        words = by_word.astype(ml_dtypes.float8_e4m3fn).view(np.uint8)
    else:
        c = by_word.astype(ml_dtypes.float4_e2m1fn).view(np.uint8) & 0xF
        words = c[..., 0::2] | (c[..., 1::2] << 4)
    return np.ascontiguousarray(words), np.ascontiguousarray(byte.astype(np.uint8).reshape(k // 512, 16, n))


def unpack_weight(words, scales, fmt):
    g, p, n, _ = words.shape
    if fmt == "e4m3":
        vals = np.ascontiguousarray(words).view(ml_dtypes.float8_e4m3fn).astype(np.float64)
    else:
        nib = np.empty((g, p, n, 4), np.uint8)
        nib[..., 0::2] = words & 0xF
        nib[..., 1::2] = words >> 4
        vals = E2M1[nib]
    vals = vals * np.repeat(np.exp2(scales.astype(np.float64) - 127.0), 8, axis=1)[..., None]
    return vals.transpose(0, 1, 3, 2).reshape(g * 512, n)
def pack4(w):
    words, scales = pack_weight(w, "e2m1")
    return words.reshape(words.shape[0], 128, -1), scales


def unpack4(words, scales):
    return unpack_weight(words.reshape(words.shape[0], 128, -1, 2), scales, "e2m1")


E4M3FN = np.array([(-1.0 if i & 128 else 1.0) * ((1.0 + (i & 7) / 8.0) * 2.0 ** (((i >> 3) & 15) - 7) if i & 120 else (i & 7) * 2.0 ** -9) for i in range(256)])


def e4m3fn_bytes(y):
    return np.clip(np.asarray(y, np.float64), -448.0, 448.0).astype(np.float32).astype(ml_dtypes.float8_e4m3fn).view(np.uint8)


def e4m3fn_values(b):
    return E4M3FN[b]


N, T, M, R, K = 512, 1024, 1024, 512, 1024


def weighted_energy(t, w):
    return np.sum(w[None, :] * np.square(t), axis=1)


def draw0():
    s, u = mx_kscale(M), mx_kscale(R)
    amp_a = np.random.uniform(0.5, 1.5, (N, 1))
    amp_x = np.random.uniform(0.5, 1.5, (T, 1))
    a = bf(np.random.standard_normal((N, M)) * amp_a * s[None, :])
    x = bf(np.random.standard_normal((T, M)) * amp_x * s[None, :])
    l_words, l_scales = pack4(np.random.standard_normal((M, R)) / np.sqrt(M) / s[:, None] * u[None, :])
    return {"a": a,
            "x": x,
            "l_words": l_words,
            "l_scales": l_scales,
            "w": bf(np.random.uniform(0.5, 1.5, (R,)) / (u * u))}


def core(a, x, l_words, l_scales, w):
    w = f64(w)
    lq = unpack4(l_words, l_scales)
    ta = mxq(f64(a), 1, "e4m3") @ lq
    tx = mxq(f64(x), 1, "e4m3") @ lq
    qa = weighted_energy(ta, w)
    qx = weighted_energy(tx, w)
    b = mxq(ta * w[None, :], 1, "e4m3") @ mxq(tx, 1, "e4m3").T
    return K * np.square(b) / (qa[:, None] * (K + qx[None, :]))


def setup_inputs():
    drawn = draw0()
    full = np.asarray(drawn['x']).astype(np.float64)
    scale = (np.abs(full).reshape(1024, 8, 128).max(axis=(2,)) / 448.0).astype(np.float32)
    given = {}
    for key, value in drawn.items():
        if key == 'x':
            given['x_bytes'] = e4m3fn_bytes(full / np.repeat(scale.astype(np.float64), 128, axis=1))
            given['x_scale'] = scale
        else:
            given[key] = value
    return given


def reference(a, x_bytes, x_scale, l_words, l_scales, w):
    return core(a, e4m3fn_values(x_bytes) * np.repeat(x_scale.astype(np.float64), 128, axis=1), l_words, l_scales, w)

@@ -1,0 +1,281 @@
+from contextlib import ExitStack
+
+import concourse.mybir as mybir
+from concourse.masks import make_identity
+
+F32 = mybir.dt.float32
+BF16 = mybir.dt.bfloat16
+U32 = mybir.dt.uint32
+I32 = mybir.dt.int32
+U8 = mybir.dt.uint8
+F8 = mybir.dt.float8_e4m3fn
+FP8X4 = mybir.dt.float8_e4m3fn_x4
+FP4X4 = mybir.dt.float4_e2m1fn_x4
+ALU = mybir.AluOpType
+ACT = mybir.ActivationFunctionType
+
+N, T, M, R, K = 512, 1024, 1024, 512, 1024
+P = 128
+FLOPS = 2 * R * M * (N + T) + 2 * N * T * R
+
+
+def tile_reducedrankkellyglrtmap_kernel(tc, a, x_bytes, x_scale, l_words, l_scales, w, out):
+    nc = tc.nc
+    seq = [("x", 0), ("a", 0), ("x", 1), ("x", 2), ("x", 3), ("a", 1), ("x", 4), ("x", 5), ("x", 6), ("x", 7), ("a", 2), ("a", 3)]
+    SD = {("x", 1), ("x", 3), ("x", 5), ("x", 7)}
+    LC, LM, LE, LD, LF, LQ = 1, 1, 2, 2, 3, 2
+    nt = len(seq)
+
+    with ExitStack() as ctx:
+        keep = ctx.enter_context(tc.tile_pool(name="keep", bufs=1))
+        work = ctx.enter_context(tc.tile_pool(name="work", bufs=3))
+        psum = ctx.enter_context(tc.psum_pool(name="psum", bufs=2))
+        ctx.enter_context(tc.manual_schedule())
+
+        ident = keep.tile([P, P], F32, name="ident")
+        lw = keep.tile([P, 2, 1024], U8, name="lw", align_bytes=64)
+        lwp = keep.tile([P, 2, 1024], U8, name="lwp", align_bytes=64)
+        ls = keep.tile([P, 2, 512], U8, name="ls", align_bytes=64)
+        lsp = keep.tile([P, 2, 512], U8, name="lsp", align_bytes=64)
+        w_rows = keep.tile([P, P], BF16, name="w_rows")
+        w_rows32 = keep.tile([P, P], F32, name="w_rows32")
+        wt = keep.tile([P, 4], F32, name="wt")
+        xs = keep.tile([P, 8, 8], F32, name="xs")
+        at = [keep.tile([P, M], BF16, name="at%d" % i, align_bytes=64) for i in range(4)]
+        xb = [keep.tile([P, M], U8, name="xb%d" % i, align_bytes=64) for i in range(8)]
+        tx_codes = keep.tile([P, T], U32, name="tx_codes", align_bytes=64)
+        tx_scales = keep.tile([P, T], U8, name="tx_scales", align_bytes=64)
+        ta_codes = keep.tile([P, N], U32, name="ta_codes", align_bytes=64)
+        ta_scales = keep.tile([P, N], U8, name="ta_scales", align_bytes=64)
+        rx = keep.tile([P, 8], F32, name="rx")
+        rqa = keep.tile([P, 4], F32, name="rqa")
+        qps = psum.tile([P, 16], F32, name="qps", tag="qps", bufs=1)
+
+        nc.vector.memset(ls[:].rearrange("p g n -> p (g n)").bitcast(I32), 0)
+        nc.vector.memset(w_rows[:], 0.0)
+        make_identity(nc, ident[:])
+
+        def load(n):
+            kind, i = seq[n]
+            if kind == "x":
+                nc.sync.dma_start(out=xb[i][:], in_=x_bytes[P * i : P * (i + 1), :])
+            else:
+                nc.sync.dma_start(out=at[i][:], in_=a[P * i : P * (i + 1), :])
+
+        nc.scalar.dma_start(out=xs[:, 0:2, :], in_=x_scale[0:256, :].rearrange("(i p) b -> p i b", p=P))
+        load(0)
+        load(1)
+        nc.sync.dma_start(out=lw[:].bitcast(I32), in_=l_words.rearrange("g p c -> p g c").bitcast(I32))
+        nc.scalar.dma_start(
+            out=w_rows[0:4, :].rearrange("t (q i) -> t q i", i=8), in_=w.rearrange("(q t i) -> t q i", t=4, i=8)
+        )
+        for q in range(4):
+            nc.scalar.dma_start(
+                out=ls[32 * q : 32 * q + 4, :, :].bitcast(I32),
+                in_=l_scales[:, 4 * q : 4 * q + 4, :].rearrange("g r n -> r g n").bitcast(I32),
+            )
+        nc.scalar.dma_start(out=xs[:, 2:8, :], in_=x_scale[256:1024, :].rearrange("(i p) b -> p i b", p=P))
+        for n in range(2, nt):
+            load(n)
+
+        words, banks, codes, mbank, sq, yb = {}, {}, {}, {}, {}, {}
+
+        def widen(n):
+            kind, i = seq[n]
+            if kind == "a":
+                return
+            xw = work.tile([P, 2, 2, 128, 2], BF16, name="xw", tag="xw")
+            words[n] = xw
+            for blk in range(8):
+                g, q = blk // 4, blk % 4
+                dst = xw[:, g, :, 32 * q : 32 * q + 32, :].rearrange("p u v e -> p v u e")
+                src = xb[i][:, 128 * blk : 128 * (blk + 1)].bitcast(F8).rearrange("p (v u e) -> p v u e", u=2, e=2)
+                nc.vector.tensor_scalar(out=dst, in0=src, scalar1=xs[:, i, blk : blk + 1], scalar2=None, op0=ALU.mult)
+        def turn(n):
+            kind, i = seq[n]
+            bank = psum.tile([P, 2, 2, 128], F32, name="tbank", tag="tbank", bufs=2)
+            banks[n] = bank
+            for g in range(2):
+                for u in range(2):
+                    if kind == "a":
+                        src = at[i][:].bitcast(F32)[:, 256 * g + u : 256 * (g + 1) : 2]
+                    else:
+                        src = words[n][:, g, u, :, :].rearrange("p v e -> p (v e)").bitcast(F32)
+                    nc.tensor.transpose(bank[:, g, u, :], src, ident[:])
+
+        def empty(n):
+            gr = work.tile([P, 2, 128, 4], BF16, name="gr", tag="gr", align_bytes=64)
+            words[n] = gr
+            nc.scalar.copy(
+                out=gr[:].rearrange("p g c t -> p (g c t)").bitcast(F32).rearrange("p (g c u) -> p g c u", g=2, u=2),
+                in_=banks[n][:].rearrange("p g u c -> p g c u"),
+            )
+
+        def quant1(n):
+            qc = work.tile([P, 256], U32, name="qc", tag="qc", align_bytes=64)
+            qs = work.tile([P, 256], U8, name="qs", tag="qs", align_bytes=64)
+            codes[n] = (qc, qs)
+            nc.vector.quantize_mx(
+                out=qc[:].bitcast(FP8X4), scales=qs[:], in_=words[n][:].rearrange("p g c t -> p (g c t)")
+            )
+
+        def project(n):
+            qc, qs = codes[n]
+            mb = psum.tile([P, 4, 128], F32, name="mbank", tag="mbank", bufs=2)
+            mbank[n] = mb
+            for t in range(4):
+                for g in range(2):
+                    nc.tensor.matmul_mx(
+                        out=mb[:, t, :],
+                        lhsT=lwp[:, g, 256 * t : 256 * (t + 1)].bitcast(FP4X4),
+                        lhsT_scale=lsp[:, g, 128 * t : 128 * (t + 1)],
+                        rhs=qc[:, 128 * g : 128 * (g + 1)].bitcast(FP8X4),
+                        rhs_scale=qs[:, 128 * g : 128 * (g + 1)],
+                        start=(g == 0),
+                        stop=(g == 1),
+                    )
+
+        def square(n):
+            s = work.tile([P, 4, 128], F32, name="sq", tag="sq")
+            sq[n] = s
+            nc.scalar.activation(out=s[:], in_=mbank[n][:], func=ACT.Square)
+
+        def second(n):
+            kind, i = seq[n]
+            y = work.tile([P, 128, 4], BF16, name="yb", tag="yb", align_bytes=64)
+            yb[n] = y
+            src = mbank[n][:].rearrange("p t c -> p c t")
+            if kind == "a":
+                nc.vector.tensor_tensor(
+                    out=y[:], in0=src, in1=wt[:].unsqueeze(1).to_broadcast([P, 128, 4]), op=ALU.mult
+                )
+            elif (kind, i) in SD:
+                nc.scalar.copy(out=y[:], in_=src)
+            else:
+                nc.vector.tensor_copy(out=y[:], in_=src)
+
+        def quant2(n):
+            kind, i = seq[n]
+            c, s = (ta_codes, ta_scales) if kind == "a" else (tx_codes, tx_scales)
+            nc.vector.quantize_mx(
+                out=c[:, 128 * i : 128 * (i + 1)].bitcast(FP8X4),
+                scales=s[:, 128 * i : 128 * (i + 1)],
+                in_=yb[n][:].rearrange("p c t -> p (c t)"),
+            )
+
+        def energy(n):
+            kind, i = seq[n]
+            col = 8 + i if kind == "a" else i
+            for t in range(4):
+                nc.tensor.matmul(
+                    out=qps[:, col : col + 1], lhsT=sq[n][:, t, :], rhs=wt[:, t : t + 1], start=(t == 0), stop=(t == 3)
+                )
+
+        def recip_a(i):
+            nc.vector.reciprocal(out=rqa[:, i : i + 1], in_=qps[:, 8 + i : 9 + i])
+
+        def recip_x(h):
+            part = rx[:, 4 * h : 4 * h + 4]
+            nc.vector.tensor_scalar(
+                out=part, in0=qps[:, 4 * h : 4 * h + 4], scalar1=1.0 / K, scalar2=1.0, op0=ALU.mult, op1=ALU.add
+            )
+            nc.vector.reciprocal(out=part, in_=part)
+
+        rxbank = {}
+
+        def spread(h):
+            bank = psum.tile([P, 4, 128], F32, name="rxbank", tag="tbank" if h else "rxbank", bufs=2 if h else 1)
+            rxbank[h] = bank
+            for c in range(4):
+                nc.tensor.transpose(
+                    bank[:, c, :], rx[:, 4 * h + c : 4 * h + c + 1].to_broadcast([P, P]), ident[:]
+                )
+
+        bb, ub = {}, {}
+
+        def cross(i, h):
+            bank = psum.tile([P, 4, 128], F32, name="bbank", tag="bbank", bufs=2)
+            bb[i, h] = bank
+            nc.tensor.matmul_mx(
+                out=bank[:].rearrange("p c n -> p (c n)"),
+                lhsT=ta_codes[:, 128 * i : 128 * (i + 1)].bitcast(FP8X4),
+                lhsT_scale=ta_scales[:, 128 * i : 128 * (i + 1)],
+                rhs=tx_codes[:, 512 * h : 512 * (h + 1)].bitcast(FP8X4),
+                rhs_scale=tx_scales[:, 512 * h : 512 * (h + 1)],
+                start=True,
+                stop=True,
+            )
+
+        def square_b(i, h):
+            u = work.tile([P, 512], F32, name="ub", tag="ub", bufs=4)
+            ub[i, h] = u
+            nc.scalar.activation(out=u[:], in_=bb[i, h][:].rearrange("p c n -> p (c n)"), func=ACT.Square)
+
+        def finish(i, h):
+            o = work.tile([P, 512], F32, name="o", tag="o", bufs=6)
+            nc.vector.scalar_tensor_tensor(
+                out=o[:], in0=ub[i, h][:], scalar=rqa[:, i : i + 1], in1=rxbank[h][:].rearrange("p c n -> p (c n)"),
+                op0=ALU.mult, op1=ALU.mult,
+            )
+            nc.sync.dma_start(out=out[P * i : P * (i + 1), 512 * h : 512 * (h + 1)], in_=o[:])
+
+        def prep_w():
+            nc.scalar.activation(out=w_rows32[:], in_=w_rows[:], func=ACT.Copy)
+            wbank = psum.tile([P, P], F32, name="wbank", tag="tbank", bufs=2)
+            nc.tensor.transpose(wbank[:], w_rows32[:], ident[:])
+            nc.vector.tensor_copy(out=wt[:], in_=wbank[:, 0:4])
+
+        def prep_l():
+            for g in range(2):
+                nc.vector.tensor_copy(
+                    out=lwp[:, g, :].bitcast(I32).rearrange("p (t q v) -> p t q v", t=4, q=16),
+                    in_=lw[:, g, :].bitcast(I32).rearrange("p (q t v) -> p t q v", t=4, q=16),
+                )
+                nc.vector.tensor_copy(
+                    out=lsp[:, g, :].bitcast(I32).rearrange("p (t q v) -> p t q v", t=4, q=16),
+                    in_=ls[:, g, :].bitcast(I32).rearrange("p (q t v) -> p t q v", t=4, q=16),
+                )
+
+        cross_at = {7: [(0, 0)], 8: [(1, 0)], 12: [(0, 1), (1, 1)], 13: [(2, 0), (2, 1)], 14: [(3, 0), (3, 1)]}
+
+        widen(0)
+        for s in range(nt + 4):
+            if 0 <= s - LE < nt:
+                square(s - LE)
+            if 0 <= s - LC < nt:
+                quant1(s - LC)
+            for n in range(nt):
+                if s - LQ - 1 == n and seq[n][0] == "a":
+                    recip_a(seq[n][1])
+            if s == 4 + LQ + 1:
+                recip_x(0)
+            if s == 9 + LQ + 1:
+                recip_x(1)
+            if s < nt:
+                turn(s)
+            if s < nt:
+                empty(s)
+            for i, h in cross_at.get(s - 1, []):
+                square_b(i, h)
+            if 0 <= s - LF < nt:
+                quant2(s - LF)
+            if s + 1 < nt:
+                widen(s + 1)
+            if s == 0:
+                prep_l()
+            if s == 1:
+                prep_w()
+            if 0 <= s - LM < nt:
+                project(s - LM)
+            if 0 <= s - LD < nt:
+                second(s - LD)
+            if s == 4 + LQ + 1:
+                spread(0)
+            if s == 9 + LQ + 1:
+                spread(1)
+            if 0 <= s - LQ < nt:
+                energy(s - LQ)
+            for i, h in cross_at.get(s - 1, []):
+                finish(i, h)
+            for i, h in cross_at.get(s, []):
+                cross(i, h)

@@ -22,15 +22,15 @@ FLOPS = 2 * R * M * (N + T) + 2 * N * T * R
 def tile_reducedrankkellyglrtmap_kernel(tc, a, x_bytes, x_scale, l_words, l_scales, w, out):
     nc = tc.nc
     seq = [("x", 0), ("a", 0), ("x", 1), ("x", 2), ("x", 3), ("a", 1), ("x", 4), ("x", 5), ("x", 6), ("x", 7), ("a", 2), ("a", 3)]
-    SD = {("x", 1), ("x", 3), ("x", 5), ("x", 7)}
-    LC, LM, LE, LD, LF, LQ = 1, 1, 2, 2, 3, 2
+    SD = {("x", i) for i in (1, 2, 3, 4, 5, 6, 7)}
+    LC, LM, LE, LD, LF, LW, LQ = 1, 2, 3, 3, 4, 4, 5
+    PRESUM = {n: 2 for n in (1, 2, 3, 4, 5, 6, 7, 8)}
     nt = len(seq)
 
     with ExitStack() as ctx:
         keep = ctx.enter_context(tc.tile_pool(name="keep", bufs=1))
-        work = ctx.enter_context(tc.tile_pool(name="work", bufs=3))
+        work = ctx.enter_context(tc.tile_pool(name="work", bufs=5))
         psum = ctx.enter_context(tc.psum_pool(name="psum", bufs=2))
-        ctx.enter_context(tc.manual_schedule())
 
         ident = keep.tile([P, P], F32, name="ident")
         lw = keep.tile([P, 2, 1024], U8, name="lw", align_bytes=64)
@@ -40,6 +40,7 @@ def tile_reducedrankkellyglrtmap_kernel(tc, a, x_bytes, x_scale, l_words, l_scal
         w_rows = keep.tile([P, P], BF16, name="w_rows")
         w_rows32 = keep.tile([P, P], F32, name="w_rows32")
         wt = keep.tile([P, 4], F32, name="wt")
+        ones = keep.tile([P, 1], F32, name="ones")
         xs = keep.tile([P, 8, 8], F32, name="xs")
         at = [keep.tile([P, M], BF16, name="at%d" % i, align_bytes=64) for i in range(4)]
         xb = [keep.tile([P, M], U8, name="xb%d" % i, align_bytes=64) for i in range(8)]
@@ -53,6 +54,7 @@ def tile_reducedrankkellyglrtmap_kernel(tc, a, x_bytes, x_scale, l_words, l_scal
 
         nc.vector.memset(ls[:].rearrange("p g n -> p (g n)").bitcast(I32), 0)
         nc.vector.memset(w_rows[:], 0.0)
+        nc.vector.memset(ones[:], 1.0)
         make_identity(nc, ident[:])
 
         def load(n):
@@ -78,19 +80,27 @@ def tile_reducedrankkellyglrtmap_kernel(tc, a, x_bytes, x_scale, l_words, l_scal
         for n in range(2, nt):
             load(n)
 
-        words, banks, codes, mbank, sq, yb = {}, {}, {}, {}, {}, {}
+        words, banks, codes, mbank, sq, yb, part = {}, {}, {}, {}, {}, {}, {}
 
         def widen(n):
             kind, i = seq[n]
             if kind == "a":
-                return
+                return []
+            ops = []
             xw = work.tile([P, 2, 2, 128, 2], BF16, name="xw", tag="xw")
             words[n] = xw
             for blk in range(8):
                 g, q = blk // 4, blk % 4
                 dst = xw[:, g, :, 32 * q : 32 * q + 32, :].rearrange("p u v e -> p v u e")
                 src = xb[i][:, 128 * blk : 128 * (blk + 1)].bitcast(F8).rearrange("p (v u e) -> p v u e", u=2, e=2)
-                nc.vector.tensor_scalar(out=dst, in0=src, scalar1=xs[:, i, blk : blk + 1], scalar2=None, op0=ALU.mult)
+                ops.append(lambda dst=dst, src=src, blk=blk: nc.vector.tensor_scalar(out=dst, in0=src, scalar1=xs[:, i, blk : blk + 1], scalar2=None, op0=ALU.mult))
+            return ops
+
+        def weave(one, two):
+            for k in range(max(len(one), len(two))):
+                for ops in (one, two):
+                    if k < len(ops):
+                        ops[k]()
         def turn(n):
             kind, i = seq[n]
             bank = psum.tile([P, 2, 2, 128], F32, name="tbank", tag="tbank", bufs=2)
@@ -163,9 +173,29 @@ def tile_reducedrankkellyglrtmap_kernel(tc, a, x_bytes, x_scale, l_words, l_scal
                 in_=yb[n][:].rearrange("p c t -> p (c t)"),
             )
 
+        def weigh(n):
+            if n not in PRESUM:
+                return []
+            s = sq[n]
+            acc = work.tile([P, 4, 128], F32, name="acc", tag="acc")
+            part[n] = acc
+            ops = []
+            for t in (0, 2):
+                ops.append(lambda t=t: nc.vector.tensor_scalar(out=acc[:, t, :], in0=s[:, t, :], scalar1=wt[:, t : t + 1], scalar2=None, op0=ALU.mult))
+            for t in (0, 2):
+                ops.append(lambda t=t: nc.vector.scalar_tensor_tensor(out=acc[:, t + 1, :], in0=s[:, t + 1, :], scalar=wt[:, t + 1 : t + 2], in1=acc[:, t, :], op0=ALU.mult, op1=ALU.add))
+            if PRESUM[n] == 1:
+                ops.append(lambda: nc.vector.tensor_tensor(out=acc[:, 0, :], in0=acc[:, 1, :], in1=acc[:, 3, :], op=ALU.add))
+            return ops
+
         def energy(n):
             kind, i = seq[n]
             col = 8 + i if kind == "a" else i
+            if n in PRESUM:
+                use = (0,) if PRESUM[n] == 1 else (1, 3)
+                for t in use:
+                    nc.tensor.matmul(out=qps[:, col : col + 1], lhsT=part[n][:, t, :], rhs=ones[:], start=(t == use[0]), stop=(t == use[-1]))
+                return
             for t in range(4):
                 nc.tensor.matmul(
                     out=qps[:, col : col + 1], lhsT=sq[n][:, t, :], rhs=wt[:, t : t + 1], start=(t == 0), stop=(t == 3)
@@ -236,10 +266,10 @@ def tile_reducedrankkellyglrtmap_kernel(tc, a, x_bytes, x_scale, l_words, l_scal
                     in_=ls[:, g, :].bitcast(I32).rearrange("p (q t v) -> p t q v", t=4, q=16),
                 )
 
-        cross_at = {7: [(0, 0)], 8: [(1, 0)], 12: [(0, 1), (1, 1)], 13: [(2, 0), (2, 1)], 14: [(3, 0), (3, 1)]}
+        cross_at = {9: [(0, 0)], 10: [(1, 0)], 14: [(0, 1), (1, 1)], 15: [(2, 0), (2, 1)], 16: [(3, 0), (3, 1)]}
 
-        widen(0)
-        for s in range(nt + 4):
+        weave(widen(0), [])
+        for s in range(nt + 6):
             if 0 <= s - LE < nt:
                 square(s - LE)
             if 0 <= s - LC < nt:
@@ -259,8 +289,7 @@ def tile_reducedrankkellyglrtmap_kernel(tc, a, x_bytes, x_scale, l_words, l_scal
                 square_b(i, h)
             if 0 <= s - LF < nt:
                 quant2(s - LF)
-            if s + 1 < nt:
-                widen(s + 1)
+            weave(widen(s + 1) if s + 1 < nt else [], weigh(s - LW) if 0 <= s - LW < nt else [])
             if s == 0:
                 prep_l()
             if s == 1:

from contextlib import ExitStack

import concourse.mybir as mybir
from concourse.masks import make_identity

F32 = mybir.dt.float32
BF16 = mybir.dt.bfloat16
U32 = mybir.dt.uint32
I32 = mybir.dt.int32
U8 = mybir.dt.uint8
F8 = mybir.dt.float8_e4m3fn
FP8X4 = mybir.dt.float8_e4m3fn_x4
FP4X4 = mybir.dt.float4_e2m1fn_x4
ALU = mybir.AluOpType
ACT = mybir.ActivationFunctionType

N, T, M, R, K = 512, 1024, 1024, 512, 1024
P = 128
FLOPS = 2 * R * M * (N + T) + 2 * N * T * R


def tile_reducedrankkellyglrtmap_kernel(tc, a, x_bytes, x_scale, l_words, l_scales, w, out):
    nc = tc.nc
    seq = [("x", 0), ("a", 0), ("x", 1), ("x", 2), ("x", 3), ("a", 1), ("x", 4), ("x", 5), ("x", 6), ("x", 7), ("a", 2), ("a", 3)]
    SD = {("x", i) for i in (1, 2, 3, 4, 5, 6, 7)}
    LC, LM, LE, LD, LF, LW, LQ = 1, 2, 3, 3, 4, 4, 5
    PRESUM = {n: 2 for n in (1, 2, 3, 4, 5, 6, 7, 8)}
    nt = len(seq)

    with ExitStack() as ctx:
        keep = ctx.enter_context(tc.tile_pool(name="keep", bufs=1))
        work = ctx.enter_context(tc.tile_pool(name="work", bufs=5))
        psum = ctx.enter_context(tc.psum_pool(name="psum", bufs=2))

        ident = keep.tile([P, P], F32, name="ident")
        lw = keep.tile([P, 2, 1024], U8, name="lw", align_bytes=64)
        lwp = keep.tile([P, 2, 1024], U8, name="lwp", align_bytes=64)
        ls = keep.tile([P, 2, 512], U8, name="ls", align_bytes=64)
        lsp = keep.tile([P, 2, 512], U8, name="lsp", align_bytes=64)
        w_rows = keep.tile([P, P], BF16, name="w_rows")
        w_rows32 = keep.tile([P, P], F32, name="w_rows32")
        wt = keep.tile([P, 4], F32, name="wt")
        ones = keep.tile([P, 1], F32, name="ones")
        xs = keep.tile([P, 8, 8], F32, name="xs")
        at = [keep.tile([P, M], BF16, name="at%d" % i, align_bytes=64) for i in range(4)]
        xb = [keep.tile([P, M], U8, name="xb%d" % i, align_bytes=64) for i in range(8)]
        tx_codes = keep.tile([P, T], U32, name="tx_codes", align_bytes=64)
        tx_scales = keep.tile([P, T], U8, name="tx_scales", align_bytes=64)
        ta_codes = keep.tile([P, N], U32, name="ta_codes", align_bytes=64)
        ta_scales = keep.tile([P, N], U8, name="ta_scales", align_bytes=64)
        rx = keep.tile([P, 8], F32, name="rx")
        rqa = keep.tile([P, 4], F32, name="rqa")
        qps = psum.tile([P, 16], F32, name="qps", tag="qps", bufs=1)

        nc.vector.memset(ls[:].rearrange("p g n -> p (g n)").bitcast(I32), 0)
        nc.vector.memset(w_rows[:], 0.0)
        nc.vector.memset(ones[:], 1.0)
        make_identity(nc, ident[:])

        def load(n):
            kind, i = seq[n]
            if kind == "x":
                nc.sync.dma_start(out=xb[i][:], in_=x_bytes[P * i : P * (i + 1), :])
            else:
                nc.sync.dma_start(out=at[i][:], in_=a[P * i : P * (i + 1), :])

        nc.scalar.dma_start(out=xs[:, 0:2, :], in_=x_scale[0:256, :].rearrange("(i p) b -> p i b", p=P))
        load(0)
        load(1)
        nc.sync.dma_start(out=lw[:].bitcast(I32), in_=l_words.rearrange("g p c -> p g c").bitcast(I32))
        nc.scalar.dma_start(
            out=w_rows[0:4, :].rearrange("t (q i) -> t q i", i=8), in_=w.rearrange("(q t i) -> t q i", t=4, i=8)
        )
        for q in range(4):
            nc.scalar.dma_start(
                out=ls[32 * q : 32 * q + 4, :, :].bitcast(I32),
                in_=l_scales[:, 4 * q : 4 * q + 4, :].rearrange("g r n -> r g n").bitcast(I32),
            )
        nc.scalar.dma_start(out=xs[:, 2:8, :], in_=x_scale[256:1024, :].rearrange("(i p) b -> p i b", p=P))
        for n in range(2, nt):
            load(n)

        words, banks, codes, mbank, sq, yb, part = {}, {}, {}, {}, {}, {}, {}

        def widen(n):
            kind, i = seq[n]
            if kind == "a":
                return []
            ops = []
            xw = work.tile([P, 2, 2, 128, 2], BF16, name="xw", tag="xw")
            words[n] = xw
            for blk in range(8):
                g, q = blk // 4, blk % 4
                dst = xw[:, g, :, 32 * q : 32 * q + 32, :].rearrange("p u v e -> p v u e")
                src = xb[i][:, 128 * blk : 128 * (blk + 1)].bitcast(F8).rearrange("p (v u e) -> p v u e", u=2, e=2)
                ops.append(lambda dst=dst, src=src, blk=blk: nc.vector.tensor_scalar(out=dst, in0=src, scalar1=xs[:, i, blk : blk + 1], scalar2=None, op0=ALU.mult))
            return ops

        def weave(one, two):
            for k in range(max(len(one), len(two))):
                for ops in (one, two):
                    if k < len(ops):
                        ops[k]()
        def turn(n):
            kind, i = seq[n]
            bank = psum.tile([P, 2, 2, 128], F32, name="tbank", tag="tbank", bufs=2)
            banks[n] = bank
            for g in range(2):
                for u in range(2):
                    if kind == "a":
                        src = at[i][:].bitcast(F32)[:, 256 * g + u : 256 * (g + 1) : 2]
                    else:
                        src = words[n][:, g, u, :, :].rearrange("p v e -> p (v e)").bitcast(F32)
                    nc.tensor.transpose(bank[:, g, u, :], src, ident[:])

        def empty(n):
            gr = work.tile([P, 2, 128, 4], BF16, name="gr", tag="gr", align_bytes=64)
            words[n] = gr
            nc.scalar.copy(
                out=gr[:].rearrange("p g c t -> p (g c t)").bitcast(F32).rearrange("p (g c u) -> p g c u", g=2, u=2),
                in_=banks[n][:].rearrange("p g u c -> p g c u"),
            )

        def quant1(n):
            qc = work.tile([P, 256], U32, name="qc", tag="qc", align_bytes=64)
            qs = work.tile([P, 256], U8, name="qs", tag="qs", align_bytes=64)
            codes[n] = (qc, qs)
            nc.vector.quantize_mx(
                out=qc[:].bitcast(FP8X4), scales=qs[:], in_=words[n][:].rearrange("p g c t -> p (g c t)")
            )

        def project(n):
            qc, qs = codes[n]
            mb = psum.tile([P, 4, 128], F32, name="mbank", tag="mbank", bufs=2)
            mbank[n] = mb
            for t in range(4):
                for g in range(2):
                    nc.tensor.matmul_mx(
                        out=mb[:, t, :],
                        lhsT=lwp[:, g, 256 * t : 256 * (t + 1)].bitcast(FP4X4),
                        lhsT_scale=lsp[:, g, 128 * t : 128 * (t + 1)],
                        rhs=qc[:, 128 * g : 128 * (g + 1)].bitcast(FP8X4),
                        rhs_scale=qs[:, 128 * g : 128 * (g + 1)],
                        start=(g == 0),
                        stop=(g == 1),
                    )

        def square(n):
            s = work.tile([P, 4, 128], F32, name="sq", tag="sq")
            sq[n] = s
            nc.scalar.activation(out=s[:], in_=mbank[n][:], func=ACT.Square)

        def second(n):
            kind, i = seq[n]
            y = work.tile([P, 128, 4], BF16, name="yb", tag="yb", align_bytes=64)
            yb[n] = y
            src = mbank[n][:].rearrange("p t c -> p c t")
            if kind == "a":
                nc.vector.tensor_tensor(
                    out=y[:], in0=src, in1=wt[:].unsqueeze(1).to_broadcast([P, 128, 4]), op=ALU.mult
                )
            elif (kind, i) in SD:
                nc.scalar.copy(out=y[:], in_=src)
            else:
                nc.vector.tensor_copy(out=y[:], in_=src)

        def quant2(n):
            kind, i = seq[n]
            c, s = (ta_codes, ta_scales) if kind == "a" else (tx_codes, tx_scales)
            nc.vector.quantize_mx(
                out=c[:, 128 * i : 128 * (i + 1)].bitcast(FP8X4),
                scales=s[:, 128 * i : 128 * (i + 1)],
                in_=yb[n][:].rearrange("p c t -> p (c t)"),
            )

        def weigh(n):
            if n not in PRESUM:
                return []
            s = sq[n]
            acc = work.tile([P, 4, 128], F32, name="acc", tag="acc")
            part[n] = acc
            ops = []
            for t in (0, 2):
                ops.append(lambda t=t: nc.vector.tensor_scalar(out=acc[:, t, :], in0=s[:, t, :], scalar1=wt[:, t : t + 1], scalar2=None, op0=ALU.mult))
            for t in (0, 2):
                ops.append(lambda t=t: nc.vector.scalar_tensor_tensor(out=acc[:, t + 1, :], in0=s[:, t + 1, :], scalar=wt[:, t + 1 : t + 2], in1=acc[:, t, :], op0=ALU.mult, op1=ALU.add))
            if PRESUM[n] == 1:
                ops.append(lambda: nc.vector.tensor_tensor(out=acc[:, 0, :], in0=acc[:, 1, :], in1=acc[:, 3, :], op=ALU.add))
            return ops

        def energy(n):
            kind, i = seq[n]
            col = 8 + i if kind == "a" else i
            if n in PRESUM:
                use = (0,) if PRESUM[n] == 1 else (1, 3)
                for t in use:
                    nc.tensor.matmul(out=qps[:, col : col + 1], lhsT=part[n][:, t, :], rhs=ones[:], start=(t == use[0]), stop=(t == use[-1]))
                return
            for t in range(4):
                nc.tensor.matmul(
                    out=qps[:, col : col + 1], lhsT=sq[n][:, t, :], rhs=wt[:, t : t + 1], start=(t == 0), stop=(t == 3)
                )

        def recip_a(i):
            nc.vector.reciprocal(out=rqa[:, i : i + 1], in_=qps[:, 8 + i : 9 + i])

        def recip_x(h):
            part = rx[:, 4 * h : 4 * h + 4]
            nc.vector.tensor_scalar(
                out=part, in0=qps[:, 4 * h : 4 * h + 4], scalar1=1.0 / K, scalar2=1.0, op0=ALU.mult, op1=ALU.add
            )
            nc.vector.reciprocal(out=part, in_=part)

        rxbank = {}

        def spread(h):
            bank = psum.tile([P, 4, 128], F32, name="rxbank", tag="tbank" if h else "rxbank", bufs=2 if h else 1)
            rxbank[h] = bank
            for c in range(4):
                nc.tensor.transpose(
                    bank[:, c, :], rx[:, 4 * h + c : 4 * h + c + 1].to_broadcast([P, P]), ident[:]
                )

        bb, ub = {}, {}

        def cross(i, h):
            bank = psum.tile([P, 4, 128], F32, name="bbank", tag="bbank", bufs=2)
            bb[i, h] = bank
            nc.tensor.matmul_mx(
                out=bank[:].rearrange("p c n -> p (c n)"),
                lhsT=ta_codes[:, 128 * i : 128 * (i + 1)].bitcast(FP8X4),
                lhsT_scale=ta_scales[:, 128 * i : 128 * (i + 1)],
                rhs=tx_codes[:, 512 * h : 512 * (h + 1)].bitcast(FP8X4),
                rhs_scale=tx_scales[:, 512 * h : 512 * (h + 1)],
                start=True,
                stop=True,
            )

        def square_b(i, h):
            u = work.tile([P, 512], F32, name="ub", tag="ub", bufs=4)
            ub[i, h] = u
            nc.scalar.activation(out=u[:], in_=bb[i, h][:].rearrange("p c n -> p (c n)"), func=ACT.Square)

        def finish(i, h):
            o = work.tile([P, 512], F32, name="o", tag="o", bufs=6)
            nc.vector.scalar_tensor_tensor(
                out=o[:], in0=ub[i, h][:], scalar=rqa[:, i : i + 1], in1=rxbank[h][:].rearrange("p c n -> p (c n)"),
                op0=ALU.mult, op1=ALU.mult,
            )
            nc.sync.dma_start(out=out[P * i : P * (i + 1), 512 * h : 512 * (h + 1)], in_=o[:])

        def prep_w():
            nc.scalar.activation(out=w_rows32[:], in_=w_rows[:], func=ACT.Copy)
            wbank = psum.tile([P, P], F32, name="wbank", tag="tbank", bufs=2)
            nc.tensor.transpose(wbank[:], w_rows32[:], ident[:])
            nc.vector.tensor_copy(out=wt[:], in_=wbank[:, 0:4])

        def prep_l():
            for g in range(2):
                nc.vector.tensor_copy(
                    out=lwp[:, g, :].bitcast(I32).rearrange("p (t q v) -> p t q v", t=4, q=16),
                    in_=lw[:, g, :].bitcast(I32).rearrange("p (q t v) -> p t q v", t=4, q=16),
                )
                nc.vector.tensor_copy(
                    out=lsp[:, g, :].bitcast(I32).rearrange("p (t q v) -> p t q v", t=4, q=16),
                    in_=ls[:, g, :].bitcast(I32).rearrange("p (q t v) -> p t q v", t=4, q=16),
                )

        cross_at = {9: [(0, 0)], 10: [(1, 0)], 14: [(0, 1), (1, 1)], 15: [(2, 0), (2, 1)], 16: [(3, 0), (3, 1)]}

        weave(widen(0), [])
        for s in range(nt + 6):
            if 0 <= s - LE < nt:
                square(s - LE)
            if 0 <= s - LC < nt:
                quant1(s - LC)
            for n in range(nt):
                if s - LQ - 1 == n and seq[n][0] == "a":
                    recip_a(seq[n][1])
            if s == 4 + LQ + 1:
                recip_x(0)
            if s == 9 + LQ + 1:
                recip_x(1)
            if s < nt:
                turn(s)
            if s < nt:
                empty(s)
            for i, h in cross_at.get(s - 1, []):
                square_b(i, h)
            if 0 <= s - LF < nt:
                quant2(s - LF)
            weave(widen(s + 1) if s + 1 < nt else [], weigh(s - LW) if 0 <= s - LW < nt else [])
            if s == 0:
                prep_l()
            if s == 1:
                prep_w()
            if 0 <= s - LM < nt:
                project(s - LM)
            if 0 <= s - LD < nt:
                second(s - LD)
            if s == 4 + LQ + 1:
                spread(0)
            if s == 9 + LQ + 1:
                spread(1)
            if 0 <= s - LQ < nt:
                energy(s - LQ)
            for i, h in cross_at.get(s - 1, []):
                finish(i, h)
            for i, h in cross_at.get(s, []):
                cross(i, h)
